import numpy as np
import ml_dtypes


def mxq(x, axis, fmt="e4m3"):
    dtype, down = {"e4m3": (ml_dtypes.float8_e4m3fn, 7), "e5m2": (ml_dtypes.float8_e5m2, 14)}[fmt]
    v = np.moveaxis(np.asarray(x, np.float32).astype(ml_dtypes.bfloat16).astype(np.float64), axis, -1)
    blocks = v.reshape(v.shape[:-1] + (-1, 32))
    amax = np.abs(blocks).max(-1, keepdims=True)
    byte = np.maximum(np.where(amax > 0, np.frexp(amax)[1] - 1 + 127, 0) - down, 1)
    scale = np.exp2(byte - 127.0)
    codes = (blocks / scale).astype(np.float32).astype(dtype).astype(np.float64)
    return np.moveaxis((codes * scale).reshape(v.shape), -1, axis)


WIDE = False


def mx_kscale(k):
    if not WIDE:
        return np.ones(k)
    levels = np.array([10, -10, 5, -5, 0])
    if k % 512:
        return np.exp2(np.random.permutation(np.resize(levels, k // 32))).repeat(32)
    a = np.empty((k // 512, 16))
    for p in range(k // 512):
        a[p, :8] = np.random.permutation(np.resize(levels, 8))
        for g in range(8):
            far = levels[np.abs(levels - a[p, g]) >= 10]
            a[p, g + 8] = far[np.random.randint(len(far))]
    return np.exp2(a.ravel()).repeat(32)


def f64(x):
    return np.asarray(x).astype(np.float64)


def striped(idx):
    return np.tile(idx.reshape(-1, 16).T, (8, 1)).astype(np.uint16)


def unstriped(offs):
    return offs[:16].T.reshape(-1).astype(np.int64)


def striped8(idx):
    return np.concatenate([x.reshape(-1, 16).T for x in idx]).astype(np.uint16)


def runs(offs, k):
    lists = np.stack([offs[16 * r : 16 * r + 16].T.reshape(-1) for r in range(8)]).astype(np.int64)
    return lists[np.arange(k) % 512 // 64]


def pack_weight(w):
    k, n = w.shape
    w = f64(np.asarray(w, np.float32).astype(ml_dtypes.bfloat16)).reshape(k // 32, 32, n)
    amax = np.abs(w).max(1)
    byte = np.clip(np.where(amax > 0, np.frexp(amax)[1] - 1 + 127 - 7, 1), 1, 254)
    scaled = (w * np.exp2(127.0 - byte)[:, None, :]).reshape(k, n).astype(np.float32)
    words = np.ascontiguousarray(scaled.reshape(k // 512, 128, 4, n).transpose(0, 1, 3, 2)).astype(ml_dtypes.float8_e4m3fn).view(np.uint8)
    return words, np.ascontiguousarray(byte.astype(np.uint8).reshape(k // 512, 16, n))


def unpack_weight(words, scales):
    g, p, n, _ = words.shape
    vals = np.ascontiguousarray(words).view(ml_dtypes.float8_e4m3fn).astype(np.float64) * np.repeat(np.exp2(scales.astype(np.float64) - 127.0), 8, axis=1)[..., None]
    return vals.transpose(0, 1, 3, 2).reshape(g * 512, n)


def relu(v):
    return np.maximum(v, 0.0)


K, T, S, N, H, W = 512, 2048, 512, 512, 512, 256


def setup_inputs():
    n = np.random.standard_normal
    s = mx_kscale(K)[:, None]
    u = mx_kscale(H)
    packed_xT = pack_weight(n((K, T)) * s)
    perm = np.stack([np.random.permutation(S) for _ in range(8)])
    return {
        "x_words": packed_xT[0],
        "x_scales": packed_xT[1],
        "w1": (n((K, H)) / np.sqrt(K) / s).astype(np.float32),
        "gn": (np.random.uniform(0.5, 1.5, (H, 1)) * u[:, None]).astype(np.float32),
        "w2": (n((H, N)) / np.sqrt(2 * H) / u[:, None]).astype(np.float32),
        "w3": (n((K, N)) / np.sqrt(2 * K) / s).astype(np.float32),
        "offs": striped(np.random.permutation(T)[:S]),
        "n1": striped8(perm[:, :W]),
        "n2": striped8(perm[:, W:]),
        "two": striped(np.random.permutation(T)[:S]),
        "n3": striped8(np.stack([np.random.permutation(S) for _ in range(8)])),
        "n4": striped8(np.stack([np.random.permutation(S) for _ in range(8)])),
    }


def reference(x_words, x_scales, w1, gn, w2, w3, offs, n1, n2, two, n3, n4):
    xq = unpack_weight(x_words, x_scales)[:, unstriped(offs)]
    y = mxq(f64(w1), 0, "e4m3").T @ xq
    pa = y[np.arange(H)[:, None], runs(n1, H)]
    pb = y[np.arange(H)[:, None], runs(n2, H)]
    rb = np.minimum(pa, pb)
    ra = np.maximum(pa, pb)
    ds = np.zeros((H, S))
    ds[np.arange(H)[:, None], runs(n1, H)] = ra
    dt = ds.copy()
    dt[np.arange(H)[:, None], runs(n2, H)] = rb
    z = f64(gn) * dt
    x_two = unpack_weight(x_words, x_scales)[:, unstriped(two)]
    h = mxq(f64(w2), 0, "e4m3").T @ mxq(z, 0, "e4m3") + mxq(f64(w3), 0, "e4m3").T @ x_two
    pa2 = h - (h[np.arange(N)[:, None], runs(n3, N)])
    pb2 = h[np.arange(N)[:, None], runs(n4, N)] - h
    return relu(np.minimum(pa2, pb2)) - (relu(-1.0 * np.maximum(pa2, pb2)))

@@ -1,0 +1,244 @@
+from contextlib import ExitStack
+
+import concourse.mybir as mybir
+
+K, T, S, N, H, W = 512, 2048, 512, 512, 512, 256
+FLOPS = 3 * 2 * 512 * 512 * 512
+
+F32 = mybir.dt.float32
+BF16 = mybir.dt.bfloat16
+I32 = mybir.dt.int32
+U32 = mybir.dt.uint32
+U16 = mybir.dt.uint16
+U8 = mybir.dt.uint8
+FP8X4 = mybir.dt.float8_e4m3fn_x4
+ALU = mybir.AluOpType
+COPY = mybir.ActivationFunctionType.Copy
+
+P = 128
+PACK = 4
+HALF = 256
+LIST_COLS = HALF // 16
+TILE_ORDER = (0, 2, 3, 1)
+
+
+def tile_picked_mixinorderminmod_none_p_kernel(
+    tc, x_words, x_scales, w1, gn, w2, w3, offs, n1, n2, two, n3, n4, out
+):
+    nc = tc.nc
+    with ExitStack() as ctx:
+        keep = ctx.enter_context(tc.tile_pool(name="keep", bufs=1))
+        ring = ctx.enter_context(tc.tile_pool(name="ring", bufs=3))
+        psum = ctx.enter_context(tc.psum_pool(name="psum", bufs=1))
+
+        def load_list(src, name):
+            tile = keep.tile(list(src.shape), U16, name=name)
+            nc.sync.dma_start(tile[:], src)
+            return tile
+
+        def load_rows(src, cols, name):
+            tile = keep.tile([P, PACK, cols.stop - cols.start], F32, name=name)
+            nc.sync.dma_start(tile[:], src.rearrange("(p j) c -> p j c", j=PACK)[:, :, cols])
+            return tile
+
+        x_table_scales = keep.tile([P, T], U8, name="x_table_scales")
+        nc.vector.memset(x_table_scales[:].bitcast(I32), 0)
+        offs_l = load_list(offs, "offs_l")
+        two_l = load_list(two, "two_l")
+        x_table_words = keep.tile([P, T], I32, name="x_table_words")
+        x_words_hbm = x_words[0].rearrange("p n t -> p (n t)").bitcast(I32)
+        nc.sync.dma_start(x_table_words[:, :HALF], x_words_hbm[:, :HALF])
+        for q in range(4):
+            nc.sync.dma_start(
+                x_table_scales[32 * q : 32 * q + 4, :].bitcast(I32),
+                x_scales[0, 4 * q : 4 * q + 4, :].bitcast(I32),
+            )
+        nc.sync.dma_start(x_table_words[:, HALF:], x_words_hbm[:, HALF:])
+        w1_raw = [load_rows(w1, slice(c, c + HALF), f"w1_raw{c}") for c in (0, HALF)]
+        n1_l = load_list(n1, "n1_l")
+        n2_l = load_list(n2, "n2_l")
+        w3_raw = load_rows(w3, slice(0, N), "w3_raw")
+        gain = keep.tile([P, PACK], F32, name="gain")
+        nc.sync.dma_start(gain[:], gn.rearrange("(p t) o -> p (t o)", t=PACK))
+        w2_raw = load_rows(w2, slice(0, N), "w2_raw")
+        n3_l = load_list(n3, "n3_l")
+        n4_l = load_list(n4, "n4_l")
+
+        def pick(lst, name):
+            scales = keep.tile([P, S], U8, name=name + "_scales", align_bytes=64)
+            words = keep.tile([P, S], U32, name=name + "_words", align_bytes=64)
+            nc.vector.tensor_copy(scales[:], x_table_scales[:].indirect(lst[:]))
+            nc.vector.tensor_copy(words[:], x_table_words[:].bitcast(U32).indirect(lst[:]))
+            return words, scales
+
+        def deal(copy, dealt, raw, raw_m0, m0, m1):
+            copy(
+                dealt[:, :, m0:m1, :].rearrange("p t m j -> p m j t"),
+                raw[:].rearrange("p j (m t) -> p m j t", t=PACK)[:, m0 - raw_m0 : m1 - raw_m0, :, :],
+            )
+
+        def weight_tiles(name):
+            dealt = keep.tile([P, PACK, P, PACK], BF16, name=name + "_dealt", align_bytes=64)
+            words = keep.tile([P, PACK * P], U32, name=name + "_words", align_bytes=64)
+            scales = keep.tile([P, PACK * P], U8, name=name + "_scales", align_bytes=64)
+            return dealt, words, scales
+
+        def quantize_weight(dealt, words, scales, t0, t1):
+            nc.vector.quantize_mx(
+                out=words[:, t0 * P : t1 * P].bitcast(FP8X4),
+                scales=scales[:, t0 * P : t1 * P],
+                in_=dealt[:, t0:t1, :, :].rearrange("p t m j -> p (t m j)"),
+            )
+
+        def product(acc, w_words, w_scales, t, a_words, a_scales, start, stop):
+            nc.tensor.matmul_mx(
+                out=acc,
+                lhsT=w_words[:, t * P : (t + 1) * P].bitcast(FP8X4),
+                lhsT_scale=w_scales[:, t * P : (t + 1) * P],
+                rhs=a_words.bitcast(FP8X4),
+                rhs_scale=a_scales,
+                start=start,
+                stop=stop,
+            )
+
+        halves = [slice(0, HALF), slice(HALF, 2 * HALF)]
+        list_halves = [slice(0, LIST_COLS), slice(LIST_COLS, 2 * LIST_COLS)]
+
+        x1_words, x1_scales = pick(offs_l, "x1")
+        x2_words, x2_scales = pick(two_l, "x2")
+
+        w1_dealt, w1_words, w1_scales = weight_tiles("w1")
+        deal(nc.scalar.copy, w1_dealt, w1_raw[0], 0, 0, 64)
+        deal(nc.scalar.copy, w1_dealt, w1_raw[1], 64, 64, 84)
+        deal(nc.vector.tensor_copy, w1_dealt, w1_raw[1], 64, 84, 128)
+        quantize_weight(w1_dealt, w1_words, w1_scales, 0, 1)
+        quantize_weight(w1_dealt, w1_words, w1_scales, 1, 4)
+
+        larger, smaller = {}, {}
+
+        def first_layer(t, first):
+            y = keep.tile([P, S], F32, name=f"y{t}")
+            if first:
+                for cols, copy in zip(halves, (nc.scalar.copy, nc.vector.tensor_copy)):
+                    acc = psum.tile([P, HALF], F32, name="y_acc", tag="y_acc", bufs=2)
+                    product(acc[:], w1_words, w1_scales, t, x1_words[:, cols], x1_scales[:, cols], True, True)
+                    copy(y[:, cols], acc[:])
+            else:
+                acc = psum.tile([P, S], F32, name="y_acc", tag="y_acc", bufs=2)
+                product(acc[:], w1_words, w1_scales, t, x1_words[:], x1_scales[:], True, True)
+                nc.scalar.copy(y[:], acc[:])
+            pa = keep.tile([P, W], F32, name=f"pa{t}")
+            pb = keep.tile([P, W], F32, name=f"pb{t}")
+            nc.scalar.activation(pa[:], y[:].indirect(n1_l[:]), COPY)
+            if first:
+                nc.vector.tensor_copy(pb[:], y[:].indirect(n2_l[:]))
+            else:
+                nc.scalar.activation(pb[:], y[:].indirect(n2_l[:]), COPY)
+            return pa, pb
+
+        pairs = {t: first_layer(t, i == 0) for i, t in enumerate(TILE_ORDER)}
+
+        def order_pair(t):
+            pa, pb = pairs[t]
+            larger[t] = keep.tile([P, W], F32, name=f"larger{t}")
+            smaller[t] = keep.tile([P, W], F32, name=f"smaller{t}")
+            nc.vector.tensor_tensor(larger[t][:], pa[:], pb[:], ALU.max)
+            nc.vector.tensor_tensor(smaller[t][:], pa[:], pb[:], ALU.min)
+
+        z_dealt = [keep.tile([P, HALF, PACK], BF16, name=f"z_dealt{c}", align_bytes=64) for c in range(2)]
+        z_words = keep.tile([P, S], U32, name="z_words", align_bytes=64)
+        z_scales = keep.tile([P, S], U8, name="z_scales", align_bytes=64)
+        placed = {}
+
+        def put_larger(t):
+            placed[t] = ring.tile([P, S], F32, name="placed", tag="placed")
+            nc.vector.tensor_copy(placed[t][:].indirect(n1_l[:]), larger[t][:])
+
+        def put_smaller(t):
+            nc.vector.tensor_copy(placed[t][:].indirect(n2_l[:]), smaller[t][:])
+
+        def gain_on_scalar(t, c):
+            nc.scalar.activation(z_dealt[c][:, :, t], placed[t][:, halves[c]], COPY, scale=gain[:, t : t + 1])
+
+        def deal_weight_on_scalar(raw, name):
+            dealt, words, scales = weight_tiles(name)
+            for m0 in range(0, P, 32):
+                deal(nc.scalar.copy, dealt, raw, 0, m0, m0 + 32)
+            return dealt, words, scales
+
+        t_a, t_b, t_c, t_d = TILE_ORDER
+        order_pair(t_a)
+        put_larger(t_a)
+        order_pair(t_b)
+        put_smaller(t_a)
+        put_larger(t_b)
+        order_pair(t_c)
+        put_smaller(t_b)
+        put_larger(t_c)
+        w3_dealt, w3_words, w3_scales = deal_weight_on_scalar(w3_raw, "w3")
+        gain_on_scalar(t_a, 0)
+        gain_on_scalar(t_a, 1)
+        quantize_weight(w3_dealt, w3_words, w3_scales, 0, 4)
+        order_pair(t_d)
+        put_smaller(t_c)
+        put_larger(t_d)
+        w2_dealt, w2_words, w2_scales = deal_weight_on_scalar(w2_raw, "w2")
+        for t in (t_b, t_c):
+            gain_on_scalar(t, 0)
+            gain_on_scalar(t, 1)
+        quantize_weight(w2_dealt, w2_words, w2_scales, 0, 4)
+        put_smaller(t_d)
+        gain_on_scalar(t_d, 0)
+        nc.vector.tensor_scalar(z_dealt[1][:, :, t_d], placed[t_d][:, halves[1]], gain[:, t_d : t_d + 1], None, ALU.mult)
+
+        accs = {}
+        for t in range(PACK):
+            if t == 0:
+                accs[t] = [psum.tile([P, HALF], F32, name=f"h_acc0{c}") for c in range(2)]
+                for c in range(2):
+                    product(accs[t][c][:], w3_words, w3_scales, t, x2_words[:, halves[c]], x2_scales[:, halves[c]], True, False)
+            else:
+                accs[t] = psum.tile([P, S], F32, name=f"h_acc{t}")
+                product(accs[t][:], w3_words, w3_scales, t, x2_words[:], x2_scales[:], True, False)
+        for c in (1, 0):
+            nc.vector.quantize_mx(
+                out=z_words[:, halves[c]].bitcast(FP8X4),
+                scales=z_scales[:, halves[c]],
+                in_=z_dealt[c][:].rearrange("p s t -> p (s t)"),
+            )
+            product(accs[0][c][:], w2_words, w2_scales, 0, z_words[:, halves[c]], z_scales[:, halves[c]], False, True)
+        for t in range(1, PACK):
+            product(accs[t][:], w2_words, w2_scales, t, z_words[:], z_scales[:], False, True)
+
+        out_rows = out.rearrange("(p t) s -> p t s", t=PACK)
+        for t in range(PACK):
+            h = keep.tile([P, S], F32, name=f"h{t}")
+            if t == 0:
+                nc.vector.tensor_copy(h[:, halves[1]], accs[0][1][:])
+                nc.scalar.copy(h[:, halves[0]], accs[0][0][:])
+            else:
+                nc.scalar.copy(h[:], accs[t][:])
+            at3 = keep.tile([P, S], F32, name=f"at3_{t}")
+            at4 = keep.tile([P, S], F32, name=f"at4_{t}")
+            for c in range(2):
+                if t == 0:
+                    nc.vector.tensor_copy(at3[:, halves[c]], h[:].indirect(n3_l[:, list_halves[c]]))
+                else:
+                    nc.scalar.activation(at3[:, halves[c]], h[:].indirect(n3_l[:, list_halves[c]]), COPY)
+                nc.scalar.activation(at4[:, halves[c]], h[:].indirect(n4_l[:, list_halves[c]]), COPY)
+            pa2 = keep.tile([P, S], F32, name=f"pa2_{t}")
+            pb2 = keep.tile([P, S], F32, name=f"pb2_{t}")
+            low = keep.tile([P, S], F32, name=f"low_{t}")
+            res = keep.tile([P, S], F32, name=f"res_{t}")
+            for cols in halves:
+                nc.vector.tensor_tensor(pa2[:, cols], h[:, cols], at3[:, cols], ALU.subtract)
+                nc.vector.tensor_tensor(pb2[:, cols], at4[:, cols], h[:, cols], ALU.subtract)
+            for cols in halves:
+                nc.vector.scalar_tensor_tensor(low[:, cols], pb2[:, cols], 0.0, pa2[:, cols], ALU.min, ALU.max)
+            for cols in halves:
+                nc.vector.scalar_tensor_tensor(res[:, cols], pb2[:, cols], 0.0, low[:, cols], ALU.max, ALU.min)
+            if t < PACK - 1:
+                nc.sync.dma_start(out_rows[:, t, :], res[:])
+            else:
+                for cols in halves:
+                    nc.sync.dma_start(out_rows[:, t, cols], res[:, cols])

@@ -37,7 +37,7 @@ def tile_picked_mixinorderminmod_none_p_kernel(
             return tile
 
         def load_rows(src, cols, name):
-            tile = keep.tile([P, PACK, cols.stop - cols.start], F32, name=name)
+            tile = keep.tile([P, PACK, cols.stop - cols.start], F32, name=name, tag=name, align_bytes=64)
             nc.sync.dma_start(tile[:], src.rearrange("(p j) c -> p j c", j=PACK)[:, :, cols])
             return tile
 
@@ -64,12 +64,15 @@ def tile_picked_mixinorderminmod_none_p_kernel(
         n3_l = load_list(n3, "n3_l")
         n4_l = load_list(n4, "n4_l")
 
-        def pick(lst, name):
-            scales = keep.tile([P, S], U8, name=name + "_scales", align_bytes=64)
-            words = keep.tile([P, S], U32, name=name + "_words", align_bytes=64)
+        def pick_scales(lst, name):
+            scales = keep.tile([P, S], U8, name=name, align_bytes=64)
             nc.vector.tensor_copy(scales[:], x_table_scales[:].indirect(lst[:]))
+            return scales
+
+        def pick_words(lst, name, tag):
+            words = keep.tile([P, S], U32, name=name, tag=tag, align_bytes=64)
             nc.vector.tensor_copy(words[:], x_table_words[:].bitcast(U32).indirect(lst[:]))
-            return words, scales
+            return words
 
         def deal(copy, dealt, raw, raw_m0, m0, m1):
             copy(
@@ -77,24 +80,24 @@ def tile_picked_mixinorderminmod_none_p_kernel(
                 raw[:].rearrange("p j (m t) -> p m j t", t=PACK)[:, m0 - raw_m0 : m1 - raw_m0, :, :],
             )
 
-        def weight_tiles(name):
-            dealt = keep.tile([P, PACK, P, PACK], BF16, name=name + "_dealt", align_bytes=64)
-            words = keep.tile([P, PACK * P], U32, name=name + "_words", align_bytes=64)
-            scales = keep.tile([P, PACK * P], U8, name=name + "_scales", align_bytes=64)
-            return dealt, words, scales
+        def dealt_tile(name):
+            return keep.tile([P, PACK, P, PACK], BF16, name=name, align_bytes=64)
 
-        def quantize_weight(dealt, words, scales, t0, t1):
+        def quantize_weight(dealt, t0, t1, name, tag):
+            words = keep.tile([P, (t1 - t0) * P], U32, name=name + "_words", tag=tag, align_bytes=64)
+            scales = keep.tile([P, (t1 - t0) * P], U8, name=name + "_scales", align_bytes=64)
             nc.vector.quantize_mx(
-                out=words[:, t0 * P : t1 * P].bitcast(FP8X4),
-                scales=scales[:, t0 * P : t1 * P],
+                out=words[:].bitcast(FP8X4),
+                scales=scales[:],
                 in_=dealt[:, t0:t1, :, :].rearrange("p t m j -> p (t m j)"),
             )
+            return {t: (words[:, (t - t0) * P : (t - t0 + 1) * P], scales[:, (t - t0) * P : (t - t0 + 1) * P]) for t in range(t0, t1)}
 
-        def product(acc, w_words, w_scales, t, a_words, a_scales, start, stop):
+        def product(acc, weight, a_words, a_scales, start, stop):
             nc.tensor.matmul_mx(
                 out=acc,
-                lhsT=w_words[:, t * P : (t + 1) * P].bitcast(FP8X4),
-                lhsT_scale=w_scales[:, t * P : (t + 1) * P],
+                lhsT=weight[0].bitcast(FP8X4),
+                lhsT_scale=weight[1],
                 rhs=a_words.bitcast(FP8X4),
                 rhs_scale=a_scales,
                 start=start,
@@ -104,36 +107,33 @@ def tile_picked_mixinorderminmod_none_p_kernel(
         halves = [slice(0, HALF), slice(HALF, 2 * HALF)]
         list_halves = [slice(0, LIST_COLS), slice(LIST_COLS, 2 * LIST_COLS)]
 
-        x1_words, x1_scales = pick(offs_l, "x1")
-        x2_words, x2_scales = pick(two_l, "x2")
+        x1_scales = pick_scales(offs_l, "x1_scales")
+        x1_words = pick_words(offs_l, "x1_words", "x1_words")
+        x2_scales = pick_scales(two_l, "x2_scales")
 
-        w1_dealt, w1_words, w1_scales = weight_tiles("w1")
+        w1_dealt = dealt_tile("w1_dealt")
         deal(nc.scalar.copy, w1_dealt, w1_raw[0], 0, 0, 64)
         deal(nc.scalar.copy, w1_dealt, w1_raw[1], 64, 64, 84)
         deal(nc.vector.tensor_copy, w1_dealt, w1_raw[1], 64, 84, 128)
-        quantize_weight(w1_dealt, w1_words, w1_scales, 0, 1)
-        quantize_weight(w1_dealt, w1_words, w1_scales, 1, 4)
+        w1_q = {**quantize_weight(w1_dealt, 0, 1, "w1_first", "w1_first"), **quantize_weight(w1_dealt, 1, 4, "w1_rest", "w1_rest")}
+        x2_words = pick_words(two_l, "x2_words", f"w1_raw{HALF}")
 
         larger, smaller = {}, {}
+        wide = {t: keep.tile([P, 2 * S], F32, name=f"wide{t}") for t in range(PACK)}
 
         def first_layer(t, first):
             y = keep.tile([P, S], F32, name=f"y{t}")
+            for cols in halves if first else [slice(0, S)]:
+                acc = psum.tile([P, cols.stop - cols.start], F32, name="y_acc", tag="y_acc", bufs=2)
+                product(acc[:], w1_q[t], x1_words[:, cols], x1_scales[:, cols], True, True)
+                nc.scalar.copy(y[:, cols], acc[:])
+            pa = wide[t][:, S : S + W]
+            pb = wide[t][:, S + W :]
+            nc.scalar.activation(pa, y[:].indirect(n1_l[:]), COPY)
             if first:
-                for cols, copy in zip(halves, (nc.scalar.copy, nc.vector.tensor_copy)):
-                    acc = psum.tile([P, HALF], F32, name="y_acc", tag="y_acc", bufs=2)
-                    product(acc[:], w1_words, w1_scales, t, x1_words[:, cols], x1_scales[:, cols], True, True)
-                    copy(y[:, cols], acc[:])
+                nc.vector.tensor_copy(pb, y[:].indirect(n2_l[:]))
             else:
-                acc = psum.tile([P, S], F32, name="y_acc", tag="y_acc", bufs=2)
-                product(acc[:], w1_words, w1_scales, t, x1_words[:], x1_scales[:], True, True)
-                nc.scalar.copy(y[:], acc[:])
-            pa = keep.tile([P, W], F32, name=f"pa{t}")
-            pb = keep.tile([P, W], F32, name=f"pb{t}")
-            nc.scalar.activation(pa[:], y[:].indirect(n1_l[:]), COPY)
-            if first:
-                nc.vector.tensor_copy(pb[:], y[:].indirect(n2_l[:]))
-            else:
-                nc.scalar.activation(pb[:], y[:].indirect(n2_l[:]), COPY)
+                nc.scalar.activation(pb, y[:].indirect(n2_l[:]), COPY)
             return pa, pb
 
         pairs = {t: first_layer(t, i == 0) for i, t in enumerate(TILE_ORDER)}
@@ -142,10 +142,10 @@ def tile_picked_mixinorderminmod_none_p_kernel(
             pa, pb = pairs[t]
             larger[t] = keep.tile([P, W], F32, name=f"larger{t}")
             smaller[t] = keep.tile([P, W], F32, name=f"smaller{t}")
-            nc.vector.tensor_tensor(larger[t][:], pa[:], pb[:], ALU.max)
-            nc.vector.tensor_tensor(smaller[t][:], pa[:], pb[:], ALU.min)
+            nc.vector.tensor_tensor(larger[t][:], pa, pb, ALU.max)
+            nc.vector.tensor_tensor(smaller[t][:], pa, pb, ALU.min)
 
-        z_dealt = [keep.tile([P, HALF, PACK], BF16, name=f"z_dealt{c}", align_bytes=64) for c in range(2)]
+        z_dealt = [keep.tile([P, HALF, PACK], BF16, name=f"z_dealt{c}", tag=f"z_dealt{c}", align_bytes=64) for c in range(2)]
         z_words = keep.tile([P, S], U32, name="z_words", align_bytes=64)
         z_scales = keep.tile([P, S], U8, name="z_scales", align_bytes=64)
         placed = {}
@@ -161,10 +161,10 @@ def tile_picked_mixinorderminmod_none_p_kernel(
             nc.scalar.activation(z_dealt[c][:, :, t], placed[t][:, halves[c]], COPY, scale=gain[:, t : t + 1])
 
         def deal_weight_on_scalar(raw, name):
-            dealt, words, scales = weight_tiles(name)
+            dealt = dealt_tile(name)
             for m0 in range(0, P, 32):
                 deal(nc.scalar.copy, dealt, raw, 0, m0, m0 + 32)
-            return dealt, words, scales
+            return dealt
 
         t_a, t_b, t_c, t_d = TILE_ORDER
         order_pair(t_a)
@@ -175,70 +175,73 @@ def tile_picked_mixinorderminmod_none_p_kernel(
         order_pair(t_c)
         put_smaller(t_b)
         put_larger(t_c)
-        w3_dealt, w3_words, w3_scales = deal_weight_on_scalar(w3_raw, "w3")
+        w3_dealt = deal_weight_on_scalar(w3_raw, "w3_dealt")
         gain_on_scalar(t_a, 0)
         gain_on_scalar(t_a, 1)
-        quantize_weight(w3_dealt, w3_words, w3_scales, 0, 4)
+        w3_q = quantize_weight(w3_dealt, 0, 1, "w3_first", "w3_first")
         order_pair(t_d)
         put_smaller(t_c)
         put_larger(t_d)
-        w2_dealt, w2_words, w2_scales = deal_weight_on_scalar(w2_raw, "w2")
+        w2_dealt = deal_weight_on_scalar(w2_raw, "w2_dealt")
         for t in (t_b, t_c):
             gain_on_scalar(t, 0)
             gain_on_scalar(t, 1)
-        quantize_weight(w2_dealt, w2_words, w2_scales, 0, 4)
+        w2_q = quantize_weight(w2_dealt, 0, 1, "w2_first", "w2_first")
         put_smaller(t_d)
-        gain_on_scalar(t_d, 0)
-        nc.vector.tensor_scalar(z_dealt[1][:, :, t_d], placed[t_d][:, halves[1]], gain[:, t_d : t_d + 1], None, ALU.mult)
+        gain_d = gain[:, t_d : t_d + 1]
+        nc.scalar.activation(z_dealt[0][:, :P, t_d], placed[t_d][:, :P], COPY, scale=gain_d)
+        nc.vector.tensor_scalar(z_dealt[1][:, :, t_d], placed[t_d][:, halves[1]], gain_d, None, ALU.mult)
+        nc.vector.tensor_scalar(z_dealt[0][:, P:, t_d], placed[t_d][:, P:HALF], gain_d, None, ALU.mult)
 
-        accs = {}
-        for t in range(PACK):
-            if t == 0:
-                accs[t] = [psum.tile([P, HALF], F32, name=f"h_acc0{c}") for c in range(2)]
-                for c in range(2):
-                    product(accs[t][c][:], w3_words, w3_scales, t, x2_words[:, halves[c]], x2_scales[:, halves[c]], True, False)
-            else:
-                accs[t] = psum.tile([P, S], F32, name=f"h_acc{t}")
-                product(accs[t][:], w3_words, w3_scales, t, x2_words[:], x2_scales[:], True, False)
+        first_accs = [psum.tile([P, HALF], F32, name=f"h_acc0{c}") for c in range(2)]
+        for c in range(2):
+            product(first_accs[c][:], w3_q[0], x2_words[:, halves[c]], x2_scales[:, halves[c]], True, False)
         for c in (1, 0):
             nc.vector.quantize_mx(
                 out=z_words[:, halves[c]].bitcast(FP8X4),
                 scales=z_scales[:, halves[c]],
                 in_=z_dealt[c][:].rearrange("p s t -> p (s t)"),
             )
-            product(accs[0][c][:], w2_words, w2_scales, 0, z_words[:, halves[c]], z_scales[:, halves[c]], False, True)
-        for t in range(1, PACK):
-            product(accs[t][:], w2_words, w2_scales, t, z_words[:], z_scales[:], False, True)
+            product(first_accs[c][:], w2_q[0], z_words[:, halves[c]], z_scales[:, halves[c]], False, True)
+            nc.scalar.copy(wide[0][:, halves[c]], first_accs[c][:])
+        w3_q.update(quantize_weight(w3_dealt, 1, 4, "w3_rest", "z_dealt1"))
+        w2_q.update(quantize_weight(w2_dealt, 1, 4, "w2_rest", "z_dealt0"))
 
         out_rows = out.rearrange("(p t) s -> p t s", t=PACK)
         for t in range(PACK):
-            h = keep.tile([P, S], F32, name=f"h{t}")
-            if t == 0:
-                nc.vector.tensor_copy(h[:, halves[1]], accs[0][1][:])
-                nc.scalar.copy(h[:, halves[0]], accs[0][0][:])
-            else:
-                nc.scalar.copy(h[:], accs[t][:])
+            last = t == PACK - 1
+            h = wide[t]
+            if t > 0:
+                acc = psum.tile([P, S], F32, name=f"h_acc{t}")
+                product(acc[:], w3_q[t], x2_words[:], x2_scales[:], True, False)
+                product(acc[:], w2_q[t], z_words[:], z_scales[:], False, True)
+                nc.scalar.copy(h[:, :S], acc[:])
             at3 = keep.tile([P, S], F32, name=f"at3_{t}")
             at4 = keep.tile([P, S], F32, name=f"at4_{t}")
-            for c in range(2):
-                if t == 0:
-                    nc.vector.tensor_copy(at3[:, halves[c]], h[:].indirect(n3_l[:, list_halves[c]]))
-                else:
-                    nc.scalar.activation(at3[:, halves[c]], h[:].indirect(n3_l[:, list_halves[c]]), COPY)
-                nc.scalar.activation(at4[:, halves[c]], h[:].indirect(n4_l[:, list_halves[c]]), COPY)
             pa2 = keep.tile([P, S], F32, name=f"pa2_{t}")
             pb2 = keep.tile([P, S], F32, name=f"pb2_{t}")
             low = keep.tile([P, S], F32, name=f"low_{t}")
             res = keep.tile([P, S], F32, name=f"res_{t}")
+            if last:
+                for c in range(2):
+                    nc.scalar.activation(at4[:, halves[c]], h[:].indirect(n4_l[:, list_halves[c]]), COPY)
+                    nc.scalar.activation(at3[:, halves[c]], h[:].indirect(n3_l[:, list_halves[c]]), COPY)
+            else:
+                nc.scalar.activation(at4[:], h[:].indirect(n4_l[:]), COPY)
+                if t == 0:
+                    nc.vector.tensor_copy(at3[:], h[:].indirect(n3_l[:]))
+                elif t == 2:
+                    nc.vector.tensor_copy(at3[:, halves[0]], h[:].indirect(n3_l[:, list_halves[0]]))
+                    nc.scalar.activation(at3[:, halves[1]], h[:].indirect(n3_l[:, list_halves[1]]), COPY)
+                else:
+                    nc.scalar.activation(at3[:], h[:].indirect(n3_l[:]), COPY)
+            for cols in halves if last else [slice(0, S)]:
+                nc.vector.tensor_tensor(pb2[:, cols], at4[:, cols], h[:, cols], ALU.subtract)
             for cols in halves:
                 nc.vector.tensor_tensor(pa2[:, cols], h[:, cols], at3[:, cols], ALU.subtract)
-                nc.vector.tensor_tensor(pb2[:, cols], at4[:, cols], h[:, cols], ALU.subtract)
             for cols in halves:
                 nc.vector.scalar_tensor_tensor(low[:, cols], pb2[:, cols], 0.0, pa2[:, cols], ALU.min, ALU.max)
             for cols in halves:
                 nc.vector.scalar_tensor_tensor(res[:, cols], pb2[:, cols], 0.0, low[:, cols], ALU.max, ALU.min)
-            if t < PACK - 1:
-                nc.sync.dma_start(out_rows[:, t, :], res[:])
-            else:
-                for cols in halves:
-                    nc.sync.dma_start(out_rows[:, t, cols], res[:, cols])
+            for cols in halves if last else [slice(0, S)]:
+                nc.sync.dma_start(out_rows[:, t, cols], res[:, cols])

from contextlib import ExitStack

import concourse.mybir as mybir

K, T, S, N, H, W = 512, 2048, 512, 512, 512, 256
FLOPS = 3 * 2 * 512 * 512 * 512

F32 = mybir.dt.float32
BF16 = mybir.dt.bfloat16
I32 = mybir.dt.int32
U32 = mybir.dt.uint32
U16 = mybir.dt.uint16
U8 = mybir.dt.uint8
FP8X4 = mybir.dt.float8_e4m3fn_x4
ALU = mybir.AluOpType
COPY = mybir.ActivationFunctionType.Copy

P = 128
PACK = 4
HALF = 256
LIST_COLS = HALF // 16
TILE_ORDER = (0, 2, 3, 1)


def tile_picked_mixinorderminmod_none_p_kernel(
    tc, x_words, x_scales, w1, gn, w2, w3, offs, n1, n2, two, n3, n4, out
):
    nc = tc.nc
    with ExitStack() as ctx:
        keep = ctx.enter_context(tc.tile_pool(name="keep", bufs=1))
        ring = ctx.enter_context(tc.tile_pool(name="ring", bufs=3))
        psum = ctx.enter_context(tc.psum_pool(name="psum", bufs=1))

        def load_list(src, name):
            tile = keep.tile(list(src.shape), U16, name=name)
            nc.sync.dma_start(tile[:], src)
            return tile

        def load_rows(src, cols, name):
            tile = keep.tile([P, PACK, cols.stop - cols.start], F32, name=name, tag=name, align_bytes=64)
            nc.sync.dma_start(tile[:], src.rearrange("(p j) c -> p j c", j=PACK)[:, :, cols])
            return tile

        x_table_scales = keep.tile([P, T], U8, name="x_table_scales")
        nc.vector.memset(x_table_scales[:].bitcast(I32), 0)
        offs_l = load_list(offs, "offs_l")
        two_l = load_list(two, "two_l")
        x_table_words = keep.tile([P, T], I32, name="x_table_words")
        x_words_hbm = x_words[0].rearrange("p n t -> p (n t)").bitcast(I32)
        nc.sync.dma_start(x_table_words[:, :HALF], x_words_hbm[:, :HALF])
        for q in range(4):
            nc.sync.dma_start(
                x_table_scales[32 * q : 32 * q + 4, :].bitcast(I32),
                x_scales[0, 4 * q : 4 * q + 4, :].bitcast(I32),
            )
        nc.sync.dma_start(x_table_words[:, HALF:], x_words_hbm[:, HALF:])
        w1_raw = [load_rows(w1, slice(c, c + HALF), f"w1_raw{c}") for c in (0, HALF)]
        n1_l = load_list(n1, "n1_l")
        n2_l = load_list(n2, "n2_l")
        w3_raw = load_rows(w3, slice(0, N), "w3_raw")
        gain = keep.tile([P, PACK], F32, name="gain")
        nc.sync.dma_start(gain[:], gn.rearrange("(p t) o -> p (t o)", t=PACK))
        w2_raw = load_rows(w2, slice(0, N), "w2_raw")
        n3_l = load_list(n3, "n3_l")
        n4_l = load_list(n4, "n4_l")

        def pick_scales(lst, name):
            scales = keep.tile([P, S], U8, name=name, align_bytes=64)
            nc.vector.tensor_copy(scales[:], x_table_scales[:].indirect(lst[:]))
            return scales

        def pick_words(lst, name, tag):
            words = keep.tile([P, S], U32, name=name, tag=tag, align_bytes=64)
            nc.vector.tensor_copy(words[:], x_table_words[:].bitcast(U32).indirect(lst[:]))
            return words

        def deal(copy, dealt, raw, raw_m0, m0, m1):
            copy(
                dealt[:, :, m0:m1, :].rearrange("p t m j -> p m j t"),
                raw[:].rearrange("p j (m t) -> p m j t", t=PACK)[:, m0 - raw_m0 : m1 - raw_m0, :, :],
            )

        def dealt_tile(name):
            return keep.tile([P, PACK, P, PACK], BF16, name=name, align_bytes=64)

        def quantize_weight(dealt, t0, t1, name, tag):
            words = keep.tile([P, (t1 - t0) * P], U32, name=name + "_words", tag=tag, align_bytes=64)
            scales = keep.tile([P, (t1 - t0) * P], U8, name=name + "_scales", align_bytes=64)
            nc.vector.quantize_mx(
                out=words[:].bitcast(FP8X4),
                scales=scales[:],
                in_=dealt[:, t0:t1, :, :].rearrange("p t m j -> p (t m j)"),
            )
            return {t: (words[:, (t - t0) * P : (t - t0 + 1) * P], scales[:, (t - t0) * P : (t - t0 + 1) * P]) for t in range(t0, t1)}

        def product(acc, weight, a_words, a_scales, start, stop):
            nc.tensor.matmul_mx(
                out=acc,
                lhsT=weight[0].bitcast(FP8X4),
                lhsT_scale=weight[1],
                rhs=a_words.bitcast(FP8X4),
                rhs_scale=a_scales,
                start=start,
                stop=stop,
            )

        halves = [slice(0, HALF), slice(HALF, 2 * HALF)]
        list_halves = [slice(0, LIST_COLS), slice(LIST_COLS, 2 * LIST_COLS)]

        x1_scales = pick_scales(offs_l, "x1_scales")
        x1_words = pick_words(offs_l, "x1_words", "x1_words")
        x2_scales = pick_scales(two_l, "x2_scales")

        w1_dealt = dealt_tile("w1_dealt")
        deal(nc.scalar.copy, w1_dealt, w1_raw[0], 0, 0, 64)
        deal(nc.scalar.copy, w1_dealt, w1_raw[1], 64, 64, 84)
        deal(nc.vector.tensor_copy, w1_dealt, w1_raw[1], 64, 84, 128)
        w1_q = {**quantize_weight(w1_dealt, 0, 1, "w1_first", "w1_first"), **quantize_weight(w1_dealt, 1, 4, "w1_rest", "w1_rest")}
        x2_words = pick_words(two_l, "x2_words", f"w1_raw{HALF}")

        larger, smaller = {}, {}
        wide = {t: keep.tile([P, 2 * S], F32, name=f"wide{t}") for t in range(PACK)}

        def first_layer(t, first):
            y = keep.tile([P, S], F32, name=f"y{t}")
            for cols in halves if first else [slice(0, S)]:
                acc = psum.tile([P, cols.stop - cols.start], F32, name="y_acc", tag="y_acc", bufs=2)
                product(acc[:], w1_q[t], x1_words[:, cols], x1_scales[:, cols], True, True)
                nc.scalar.copy(y[:, cols], acc[:])
            pa = wide[t][:, S : S + W]
            pb = wide[t][:, S + W :]
            nc.scalar.activation(pa, y[:].indirect(n1_l[:]), COPY)
            if first:
                nc.vector.tensor_copy(pb, y[:].indirect(n2_l[:]))
            else:
                nc.scalar.activation(pb, y[:].indirect(n2_l[:]), COPY)
            return pa, pb

        pairs = {t: first_layer(t, i == 0) for i, t in enumerate(TILE_ORDER)}

        def order_pair(t):
            pa, pb = pairs[t]
            larger[t] = keep.tile([P, W], F32, name=f"larger{t}")
            smaller[t] = keep.tile([P, W], F32, name=f"smaller{t}")
            nc.vector.tensor_tensor(larger[t][:], pa, pb, ALU.max)
            nc.vector.tensor_tensor(smaller[t][:], pa, pb, ALU.min)

        z_dealt = [keep.tile([P, HALF, PACK], BF16, name=f"z_dealt{c}", tag=f"z_dealt{c}", align_bytes=64) for c in range(2)]
        z_words = keep.tile([P, S], U32, name="z_words", align_bytes=64)
        z_scales = keep.tile([P, S], U8, name="z_scales", align_bytes=64)
        placed = {}

        def put_larger(t):
            placed[t] = ring.tile([P, S], F32, name="placed", tag="placed")
            nc.vector.tensor_copy(placed[t][:].indirect(n1_l[:]), larger[t][:])

        def put_smaller(t):
            nc.vector.tensor_copy(placed[t][:].indirect(n2_l[:]), smaller[t][:])

        def gain_on_scalar(t, c):
            nc.scalar.activation(z_dealt[c][:, :, t], placed[t][:, halves[c]], COPY, scale=gain[:, t : t + 1])

        def deal_weight_on_scalar(raw, name):
            dealt = dealt_tile(name)
            for m0 in range(0, P, 32):
                deal(nc.scalar.copy, dealt, raw, 0, m0, m0 + 32)
            return dealt

        t_a, t_b, t_c, t_d = TILE_ORDER
        order_pair(t_a)
        put_larger(t_a)
        order_pair(t_b)
        put_smaller(t_a)
        put_larger(t_b)
        order_pair(t_c)
        put_smaller(t_b)
        put_larger(t_c)
        w3_dealt = deal_weight_on_scalar(w3_raw, "w3_dealt")
        gain_on_scalar(t_a, 0)
        gain_on_scalar(t_a, 1)
        w3_q = quantize_weight(w3_dealt, 0, 1, "w3_first", "w3_first")
        order_pair(t_d)
        put_smaller(t_c)
        put_larger(t_d)
        w2_dealt = deal_weight_on_scalar(w2_raw, "w2_dealt")
        for t in (t_b, t_c):
            gain_on_scalar(t, 0)
            gain_on_scalar(t, 1)
        w2_q = quantize_weight(w2_dealt, 0, 1, "w2_first", "w2_first")
        put_smaller(t_d)
        gain_d = gain[:, t_d : t_d + 1]
        nc.scalar.activation(z_dealt[0][:, :P, t_d], placed[t_d][:, :P], COPY, scale=gain_d)
        nc.vector.tensor_scalar(z_dealt[1][:, :, t_d], placed[t_d][:, halves[1]], gain_d, None, ALU.mult)
        nc.vector.tensor_scalar(z_dealt[0][:, P:, t_d], placed[t_d][:, P:HALF], gain_d, None, ALU.mult)

        first_accs = [psum.tile([P, HALF], F32, name=f"h_acc0{c}") for c in range(2)]
        for c in range(2):
            product(first_accs[c][:], w3_q[0], x2_words[:, halves[c]], x2_scales[:, halves[c]], True, False)
        for c in (1, 0):
            nc.vector.quantize_mx(
                out=z_words[:, halves[c]].bitcast(FP8X4),
                scales=z_scales[:, halves[c]],
                in_=z_dealt[c][:].rearrange("p s t -> p (s t)"),
            )
            product(first_accs[c][:], w2_q[0], z_words[:, halves[c]], z_scales[:, halves[c]], False, True)
            nc.scalar.copy(wide[0][:, halves[c]], first_accs[c][:])
        w3_q.update(quantize_weight(w3_dealt, 1, 4, "w3_rest", "z_dealt1"))
        w2_q.update(quantize_weight(w2_dealt, 1, 4, "w2_rest", "z_dealt0"))

        out_rows = out.rearrange("(p t) s -> p t s", t=PACK)
        for t in range(PACK):
            last = t == PACK - 1
            h = wide[t]
            if t > 0:
                acc = psum.tile([P, S], F32, name=f"h_acc{t}")
                product(acc[:], w3_q[t], x2_words[:], x2_scales[:], True, False)
                product(acc[:], w2_q[t], z_words[:], z_scales[:], False, True)
                nc.scalar.copy(h[:, :S], acc[:])
            at3 = keep.tile([P, S], F32, name=f"at3_{t}")
            at4 = keep.tile([P, S], F32, name=f"at4_{t}")
            pa2 = keep.tile([P, S], F32, name=f"pa2_{t}")
            pb2 = keep.tile([P, S], F32, name=f"pb2_{t}")
            low = keep.tile([P, S], F32, name=f"low_{t}")
            res = keep.tile([P, S], F32, name=f"res_{t}")
            if last:
                for c in range(2):
                    nc.scalar.activation(at4[:, halves[c]], h[:].indirect(n4_l[:, list_halves[c]]), COPY)
                    nc.scalar.activation(at3[:, halves[c]], h[:].indirect(n3_l[:, list_halves[c]]), COPY)
            else:
                nc.scalar.activation(at4[:], h[:].indirect(n4_l[:]), COPY)
                if t == 0:
                    nc.vector.tensor_copy(at3[:], h[:].indirect(n3_l[:]))
                elif t == 2:
                    nc.vector.tensor_copy(at3[:, halves[0]], h[:].indirect(n3_l[:, list_halves[0]]))
                    nc.scalar.activation(at3[:, halves[1]], h[:].indirect(n3_l[:, list_halves[1]]), COPY)
                else:
                    nc.scalar.activation(at3[:], h[:].indirect(n3_l[:]), COPY)
            for cols in halves if last else [slice(0, S)]:
                nc.vector.tensor_tensor(pb2[:, cols], at4[:, cols], h[:, cols], ALU.subtract)
            for cols in halves:
                nc.vector.tensor_tensor(pa2[:, cols], h[:, cols], at3[:, cols], ALU.subtract)
            for cols in halves:
                nc.vector.scalar_tensor_tensor(low[:, cols], pb2[:, cols], 0.0, pa2[:, cols], ALU.min, ALU.max)
            for cols in halves:
                nc.vector.scalar_tensor_tensor(res[:, cols], pb2[:, cols], 0.0, low[:, cols], ALU.max, ALU.min)
            for cols in halves if last else [slice(0, S)]:
                nc.sync.dma_start(out_rows[:, t, cols], res[:, cols])
